import numpy as np
import ml_dtypes


def mxq(x, axis, fmt="e4m3"):
    dtype, down = {"e4m3": (ml_dtypes.float8_e4m3fn, 7), "e5m2": (ml_dtypes.float8_e5m2, 14)}[fmt]
    v = np.moveaxis(np.asarray(x, np.float32).astype(ml_dtypes.bfloat16).astype(np.float64), axis, -1)
    blocks = v.reshape(v.shape[:-1] + (-1, 32))
    amax = np.abs(blocks).max(-1, keepdims=True)
    byte = np.maximum(np.where(amax > 0, np.frexp(amax)[1] - 1 + 127, 0) - down, 1)
    scale = np.exp2(byte - 127.0)
    codes = (blocks / scale).astype(np.float32).astype(dtype).astype(np.float64)
    return np.moveaxis((codes * scale).reshape(v.shape), -1, axis)


WIDE = False


def mx_kscale(k):
    if not WIDE:
        return np.ones(k)
    levels = np.array([10, -10, 5, -5, 0])
    if k % 512:
        return np.exp2(np.random.permutation(np.resize(levels, k // 32))).repeat(32)
    a = np.empty((k // 512, 16))
    for p in range(k // 512):
        a[p, :8] = np.random.permutation(np.resize(levels, 8))
        for g in range(8):
            far = levels[np.abs(levels - a[p, g]) >= 10]
            a[p, g + 8] = far[np.random.randint(len(far))]
    return np.exp2(a.ravel()).repeat(32)


def f64(x):
    return np.asarray(x).astype(np.float64)


def striped(idx):
    return np.tile(np.asarray(idx).reshape(-1, 16).T, (8, 1)).astype(np.uint16)


def unstriped(offs):
    return offs[:16].T.reshape(-1).astype(np.int64)


E2M1 = np.array([0.0, 0.5, 1.0, 1.5, 2.0, 3.0, 4.0, 6.0, -0.0, -0.5, -1.0, -1.5, -2.0, -3.0, -4.0, -6.0])


def pack_weight(w, fmt):
    k, n = w.shape
    w = f64(np.asarray(w, np.float32).astype(ml_dtypes.bfloat16)).reshape(k // 32, 32, n)
    amax = np.abs(w).max(1)
    if fmt == "e4m3":
        byte = np.frexp(amax)[1] - 1 + 127 - 7
    else:
        mant, ex = np.frexp(amax / 6.0)
        byte = np.where(mant > 0.5, ex, ex - 1) + 127
    byte = np.clip(np.where(amax > 0, byte, 1), 1, 254)
    scaled = (w * np.exp2(127.0 - byte)[:, None, :]).reshape(k, n).astype(np.float32)
    by_word = np.ascontiguousarray(scaled.reshape(k // 512, 128, 4, n).transpose(0, 1, 3, 2))
    if fmt == "e4m3":
        words = by_word.astype(ml_dtypes.float8_e4m3fn).view(np.uint8)
    else:
        c = by_word.astype(ml_dtypes.float4_e2m1fn).view(np.uint8) & 0xF
        words = (c[..., 0::2] | (c[..., 1::2] << 4)).reshape(k // 512, 128, 2 * n)
    return np.ascontiguousarray(words), np.ascontiguousarray(byte.astype(np.uint8).reshape(k // 512, 16, n))


def unpack_weight(words, scales, fmt):
    g, _, n = scales.shape
    words = np.ascontiguousarray(words).reshape(g, 128, n, -1)
    if fmt == "e4m3":
        vals = words.view(ml_dtypes.float8_e4m3fn).astype(np.float64)
    else:
        nib = np.empty((g, 128, n, 4), np.uint8)
        nib[..., 0::2] = words & 0xF
        nib[..., 1::2] = words >> 4
        vals = E2M1[nib]
    vals = vals * np.repeat(np.exp2(scales.astype(np.float64) - 127.0), 8, axis=1)[..., None]
    return vals.transpose(0, 1, 3, 2).reshape(g * 512, n)


def sigmoid(v):
    return 1.0 / (1.0 + np.exp(-v))


D, K, R, T, I, Q, G, U = 512, 512, 512, 2048, 512, 128, 64, 1024


def setup_inputs():
    n = np.random.standard_normal
    idx2 = np.random.permutation(U)[:I]
    idx = np.random.permutation(T)[:I]
    fd = mx_kscale(D)
    fk = mx_kscale(K)
    fr = mx_kscale(R)
    keysp = pack_weight(n((D, T)) / fd[:, None], "e4m3")
    tabp = pack_weight(n((K, T)) / fk[:, None], "e4m3")
    return {
        "query": (n((D, Q)) * 0.6 / np.sqrt(D) * fd[:, None]).astype(np.float32),
        "keys_words": keysp[0],
        "keys_scales": keysp[1],
        "sharp": (np.random.uniform(1.0, 3.0, (Q, 1))).astype(np.float32),
        "tab_words": tabp[0],
        "tab_scales": tabp[1],
        "w1": (n((K, R)) * 1 / np.sqrt(K) * fk[:, None]).astype(np.float32),
        "gtab": (n((R, U))).astype(np.float32),
        "gout": (n((R, Q)) * 1 / np.sqrt(R) * fr[:, None]).astype(np.float32),
        "hsc": (np.random.uniform(0.7, 1.4, (R, 1)) / fr[:, None]).astype(np.float32),
        "old": (0.5 * n((Q, T))).astype(np.float32),
        "offs2": striped(idx2),
        "offs": striped(idx),
    }


def reference(query, keys_words, keys_scales, sharp, tab_words, tab_scales, w1, gtab, gout, hsc, old, offs2, offs):
    idx2 = unstriped(offs2)
    idx = unstriped(offs)
    keysu = unpack_weight(keys_words, keys_scales, "e4m3")
    tabu = unpack_weight(tab_words, tab_scales, "e4m3")
    queryq = mxq(f64(query), 0, "e4m3")
    keysidxg = keysu[:, idx]
    a = queryq.T @ keysidxg
    p = np.exp(a)
    s = p.reshape(Q, G, I // G).sum(axis=2)
    ms = a.reshape(Q, G, I // G).mean(axis=2) * f64(sharp)
    pg = np.exp(ms - np.max(ms, axis=1, keepdims=True))
    z = np.sum(pg, axis=1, keepdims=True)
    sh = pg / z / s
    rr = np.repeat(sh, I // G, axis=1)
    w1q = mxq(f64(w1), 0, "e4m3")
    tabidxg = tabu[:, idx]
    zh = w1q.T @ tabidxg
    hg = sigmoid(f64(gtab)[:, idx2])
    hv = zh * hg
    hs1 = hv * f64(hsc)
    goutq = mxq(f64(gout), 0, "e4m3")
    hs1q = mxq(hs1, 0, "e4m3")
    c0 = goutq.T @ hs1q
    drr = c0 * p
    dsh = drr.reshape(Q, G, I // G).sum(axis=2)
    dz = np.sum(dsh / s * pg / np.square(z) * (-1.0), axis=1, keepdims=True)
    dpg = dsh / s / z + dz
    dms = dpg * pg
    e1 = dms * f64(sharp) / 8.0
    r1 = np.repeat(e1, I // G, axis=1)
    ds = dsh * pg / z / np.square(s) * (-1.0)
    r2 = np.repeat(ds, I // G, axis=1)
    dp = c0 * rr + r2
    da = r1 + dp * p
    gs = da * 512.0
    gf = np.zeros((Q, T))
    gf[:, idx] = gs
    y = f64(old) + gf
    return y

@@ -1,0 +1,214 @@
+from contextlib import ExitStack
+
+import concourse.mybir as mybir
+
+F32 = mybir.dt.float32
+BF16 = mybir.dt.bfloat16
+I32 = mybir.dt.int32
+U32 = mybir.dt.uint32
+U16 = mybir.dt.uint16
+U8 = mybir.dt.uint8
+FP8X4 = mybir.dt.float8_e4m3fn_x4
+ALU = mybir.AluOpType
+ACT = mybir.ActivationFunctionType
+AXIS_X = mybir.AxisListType.X
+
+P = 128
+PACK = 4
+D, K, R, T, I, Q, G, U = 512, 512, 512, 2048, 512, 128, 64, 1024
+GROUP = I // G
+HALF = I // 2
+OUT_CHUNKS = (640, 640, 512, 256)
+TAB_PLANE_ROW = 4
+
+FLOPS = 2 * (D * Q * I + K * R * I + R * Q * I)
+
+
+def tile_attend_blrgated_bygroup_kernel(
+    tc, query, keys_words, keys_scales, sharp, tab_words, tab_scales, w1, gtab, gout, hsc, old, offs2, offs, out
+):
+    nc = tc.nc
+    with ExitStack() as ctx:
+        sb = ctx.enter_context(tc.tile_pool(name="sb", bufs=1))
+        ps = ctx.enter_context(tc.psum_pool(name="ps", bufs=1))
+
+        def tile(name, shape, dtype, tag=None):
+            return sb.tile(shape, dtype, name=name, tag=tag or name, align_bytes=64)
+
+        def by_group(ap):
+            return ap.rearrange("p (g j) -> p g j", j=GROUP)
+
+        def spread(ap, groups):
+            return ap.unsqueeze(2).to_broadcast([P, groups, GROUP])
+
+        def quantize(name, grouped, width, tag=None):
+            codes = tile(name + "_codes", [P, width], U32, tag=tag)
+            scales = tile(name + "_scales", [P, width], U8)
+            nc.vector.quantize_mx(out=codes[:].bitcast(FP8X4), scales=scales[:], in_=grouped)
+            return codes, scales
+
+        offs_sb = sb.tile([P, I // 16], U16, name="offs_sb")
+        offs2_sb = sb.tile([P, I // 16], U16, name="offs2_sb")
+        key_words = tile("key_words", [P, T], I32)
+        tab_words_sb = tile("tab_words_sb", [P, T], I32)
+        key_scales = tile("key_scales", [P, T], U8)
+        tab_scales_sb = tile("tab_scales_sb", [P, T], U8)
+        query_raw = tile("query_raw", [P, PACK, Q], F32)
+        gout_raw = tile("gout_raw", [P, PACK, Q], F32)
+        w1_raw = tile("w1_raw", [P, PACK, R], F32)
+        gates = [tile("gates%d" % t, [P, U], F32) for t in range(PACK)]
+        old_sb = tile("old_sb", [P, T], F32)
+        sharp_sb = tile("sharp_sb", [P, 1], F32)
+        hsc_sb = tile("hsc_sb", [P, PACK], F32)
+
+        nc.vector.memset(tab_scales_sb[:].bitcast(I32), 0)
+        nc.vector.memset(key_scales[:].bitcast(I32), 0)
+
+        gtab_planes = gtab.rearrange("(p t) u -> t p u", t=PACK)
+        w1_rows = w1.rearrange("(p j) c -> p j c", j=PACK)
+        nc.sync.dma_start(w1_raw[:, 0, :], w1_rows[:, 0, :])
+        nc.scalar.dma_start(hsc_sb[:], hsc.rearrange("(p t) o -> p (t o)", t=PACK))
+        nc.sync.dma_start(offs_sb[:], offs)
+        nc.scalar.dma_start(sharp_sb[:], sharp)
+        nc.sync.dma_start(offs2_sb[:], offs2)
+        for j in range(1, PACK):
+            nc.sync.dma_start(w1_raw[:, j, :], w1_rows[:, j, :])
+        for f in range(4):
+            nc.sync.dma_start(
+                tab_scales_sb[TAB_PLANE_ROW + f : P : 32, :].bitcast(I32), tab_scales[0, f:16:4, :].bitcast(I32)
+            )
+        nc.sync.dma_start(tab_words_sb[:], tab_words[0].rearrange("p n t -> p (n t)").bitcast(I32))
+        for f in range(4):
+            nc.sync.dma_start(key_scales[f:P:32, :].bitcast(I32), keys_scales[0, f:16:4, :].bitcast(I32))
+        for t in range(PACK):
+            nc.sync.dma_start(gates[t][:], gtab_planes[t])
+        nc.sync.dma_start(gout_raw[:], gout.rearrange("(p j) c -> p j c", j=PACK))
+        nc.sync.dma_start(query_raw[:], query.rearrange("(p j) c -> p j c", j=PACK))
+        nc.sync.dma_start(key_words[:], keys_words[0].rearrange("p n t -> p (n t)").bitcast(I32))
+        nc.sync.dma_start(old_sb[:], old)
+
+        sharp8 = tile("sharp8", [P, 1], F32)
+        neg_sharp8 = tile("neg_sharp8", [P, 1], F32)
+        nc.scalar.activation(sharp8[:], sharp_sb[:], ACT.Copy, scale=1.0 / GROUP)
+        nc.scalar.activation(neg_sharp8[:], sharp_sb[:], ACT.Copy, scale=-1.0 / GROUP)
+
+        w1_bf = tile("w1_bf", [P, PACK, P, PACK], BF16)
+        nc.scalar.activation(
+            w1_bf[:].rearrange("p t m j -> p m t j"), w1_raw[:].rearrange("p j (m t) -> p m t j", t=PACK), ACT.Copy
+        )
+        tab_w = tile("tab_w", [P, I], U32)
+        tab_s = tile("tab_s", [P, I], U8)
+        nc.vector.tensor_copy(tab_s[:], tab_scales_sb[:].indirect(offs_sb[:]))
+        nc.vector.tensor_copy(tab_w[:], tab_words_sb[:].bitcast(U32).indirect(offs_sb[:]))
+        w1_codes, w1_scales = quantize("w1", w1_bf[:].rearrange("p t m j -> p (t m j)"), R, "tab_words_sb")
+        zh = [ps.tile([P, I], F32, name="zh%d" % t) for t in range(PACK)]
+        for t in range(PACK):
+            cols = slice(t * P, (t + 1) * P)
+            nc.tensor.matmul_mx(
+                out=zh[t][:], lhsT=w1_codes[:, cols].bitcast(FP8X4), lhsT_scale=w1_scales[:, cols],
+                rhs=tab_w[:].bitcast(FP8X4), rhs_scale=tab_s[TAB_PLANE_ROW:P, :], start=True, stop=True,
+            )
+
+        pairs = tile("pairs", [P, 2, I, 2], BF16)
+        for t in range(PACK):
+            hg = tile("hg%d" % t, [P, I], F32)
+            nc.scalar.activation(hg[:], gates[t][:].indirect(offs2_sb[:]), ACT.Sigmoid)
+            nc.vector.scalar_tensor_tensor(
+                pairs[:, t // 2, :, t % 2], zh[t][:], hsc_sb[:, t : t + 1], hg[:], ALU.mult, ALU.mult
+            )
+        window = tile("window", [P, T], F32, tag="gates0")
+        nc.gpsimd.memset(window[:], 0.0)
+        key_s = tile("key_s", [P, I], U8, tag="w1_bf")
+        nc.vector.tensor_copy(key_s[:], key_scales[:].indirect(offs_sb[:]))
+
+        hs_words = tile("hs_words", [P, I, 2], I32)
+        pair_words = pairs[:].rearrange("p a n e -> p (a n e)").bitcast(I32)
+        nc.vector.tensor_copy(hs_words[:], pair_words.rearrange("p (a n) -> p n a", a=2))
+        hs_codes, hs_scales = quantize("hs", hs_words[:].rearrange("p n a -> p (n a)").bitcast(BF16), I)
+
+        gout_bf = tile("gout_bf", [P, Q, PACK], BF16, tag="gates1")
+        nc.gpsimd.tensor_scalar(gout_bf[:], gout_raw[:].rearrange("p j c -> p c j"), 1.0, 0.0, ALU.mult, ALU.add)
+        query_bf = tile("query_bf", [P, Q, PACK], BF16, tag="gout_raw")
+        nc.gpsimd.tensor_scalar(query_bf[:], query_raw[:].rearrange("p j c -> p c j"), 1.0, 0.0, ALU.mult, ALU.add)
+        gout_codes, gout_scales = quantize("gout", gout_bf[:].rearrange("p c j -> p (c j)"), Q, "hg3")
+        query_codes, query_scales = quantize("query", query_bf[:].rearrange("p c j -> p (c j)"), Q, "hg2")
+        c0 = ps.tile([P, I], F32, name="c0")
+        nc.tensor.matmul_mx(
+            out=c0[:], lhsT=gout_codes[:].bitcast(FP8X4), lhsT_scale=gout_scales[:],
+            rhs=hs_codes[:].bitcast(FP8X4), rhs_scale=hs_scales[:], start=True, stop=True,
+        )
+
+        halves = [slice(h * HALF, (h + 1) * HALF) for h in range(2)]
+        group_halves = [slice(h * G // 2, (h + 1) * G // 2) for h in range(2)]
+        a_ps = []
+        for h, tag in enumerate(("pairs", "hs_words")):
+            key_w = tile("key_w%d" % h, [P, HALF], U32, tag=tag)
+            listed = offs_sb[:, h * HALF // 16 : (h + 1) * HALF // 16]
+            nc.vector.tensor_copy(key_w[:], key_words[:].bitcast(U32).indirect(listed))
+            a_ps.append(ps.tile([P, HALF], F32, name="a_ps%d" % h))
+            nc.tensor.matmul_mx(
+                out=a_ps[h][:], lhsT=query_codes[:].bitcast(FP8X4), lhsT_scale=query_scales[:],
+                rhs=key_w[:].bitcast(FP8X4), rhs_scale=key_s[:, halves[h]], start=True, stop=True,
+            )
+        a_sum = tile("a_sum", [P, G], F32)
+        p_sb = tile("p_sb", [P, I], F32)
+        s = tile("s", [P, G], F32)
+        inv_s = tile("inv_s", [P, G], F32)
+        pn = tile("pn", [P, I], F32)
+        d = tile("d", [P, I], F32)
+        m = tile("m", [P, G], F32)
+        y = tile("y", [P, I], F32)
+        inner = tile("inner", [P, I], F32)
+        both = list(zip(halves, group_halves))
+        for h, (slots, groups) in enumerate(both):
+            nc.scalar.activation(p_sb[:, slots], a_ps[h][:], ACT.Exp)
+            nc.vector.tensor_reduce(a_sum[:, groups], by_group(a_ps[h][:]), AXIS_X, ALU.add)
+        neg_ms = tile("neg_ms", [P, G], F32)
+        neg_max = tile("neg_max", [P, 1], F32)
+        nc.vector.tensor_reduce(s[:, group_halves[0]], by_group(p_sb[:, halves[0]]), AXIS_X, ALU.add)
+        nc.vector.tensor_scalar(neg_ms[:], a_sum[:], neg_sharp8[:], None, ALU.mult, ALU.min, accum_out=neg_max[:])
+        nc.vector.tensor_reduce(s[:, group_halves[1]], by_group(p_sb[:, halves[1]]), AXIS_X, ALU.add)
+        pg = tile("pg", [P, G], F32)
+        z = tile("z", [P, 1], F32)
+        nc.scalar.activation(pg[:], neg_ms[:], ACT.Exp, bias=neg_max[:], scale=-1.0, accum_out=z[:])
+        inv_z = tile("inv_z", [P, 1], F32)
+        for slots, groups in both:
+            nc.vector.reciprocal(inv_s[:, groups], s[:, groups])
+        nc.vector.reciprocal(inv_z[:], z[:])
+        w_slots = tile("w_slots", [P, I], F32)
+        nc.scalar.activation(by_group(w_slots[:]), spread(pg[:], G), ACT.Copy, scale=inv_z[:])
+        for slots, groups in both:
+            nc.vector.tensor_tensor(
+                by_group(pn[:, slots]), by_group(p_sb[:, slots]), spread(inv_s[:, groups], G // 2), ALU.mult
+            )
+
+        for slots, groups in both:
+            nc.vector.scalar_tensor_tensor(d[:, slots], c0[:, slots], -512.0, pn[:, slots], ALU.mult, ALU.mult)
+        for slots, groups in both:
+            nc.vector.tensor_reduce(m[:, groups], by_group(d[:, slots]), AXIS_X, ALU.add)
+        wm = tile("wm", [P, G], F32)
+        mean8 = tile("mean8", [P, 1], F32)
+
+        def centre(slots, groups):
+            nc.vector.scalar_tensor_tensor(
+                by_group(y[:, slots]), by_group(pn[:, slots]), sharp8[:], spread(m[:, groups], G // 2),
+                ALU.subtract, ALU.mult,
+            )
+
+        centre(*both[0])
+        nc.vector.scalar_tensor_tensor(
+            wm[:], m[:], sharp8[:], w_slots[:, 0:I:GROUP], ALU.mult, ALU.mult, accum_out=mean8[:]
+        )
+        centre(*both[1])
+        for slots, groups in both:
+            nc.vector.scalar_tensor_tensor(inner[:, slots], y[:, slots], mean8[:], d[:, slots], ALU.add, ALU.subtract)
+        nc.vector.tensor_tensor(window[:].indirect(offs_sb[:]), inner[:], w_slots[:], ALU.mult)
+
+        start = 0
+        for c, width in enumerate(OUT_CHUNKS):
+            cols = slice(start, start + width)
+            start = start + width
+            result = tile("result%d" % c, [P, width], F32)
+            nc.vector.tensor_tensor(result[:], window[:, cols], old_sb[:, cols], ALU.add)
+            queue = nc.sync if c % 2 == 0 else nc.scalar
+            queue.dma_start(out[:, cols], result[:])

@@ -19,6 +19,7 @@ D, K, R, T, I, Q, G, U = 512, 512, 512, 2048, 512, 128, 64, 1024
 GROUP = I // G
 HALF = I // 2
 OUT_CHUNKS = (640, 640, 512, 256)
+KEY_LOADS = (0, 768, 1408, 2048)
 TAB_PLANE_ROW = 4
 
 FLOPS = 2 * (D * Q * I + K * R * I + R * Q * I)
@@ -61,46 +62,89 @@ def tile_attend_blrgated_bygroup_kernel(
         sharp_sb = tile("sharp_sb", [P, 1], F32)
         hsc_sb = tile("hsc_sb", [P, PACK], F32)
 
-        nc.vector.memset(tab_scales_sb[:].bitcast(I32), 0)
+        window = tile("window", [P, T], F32)
         nc.vector.memset(key_scales[:].bitcast(I32), 0)
+        nc.vector.memset(tab_scales_sb[:].bitcast(I32), 0)
+        nc.vector.memset(window[:], 0.0)
 
         gtab_planes = gtab.rearrange("(p t) u -> t p u", t=PACK)
-        w1_rows = w1.rearrange("(p j) c -> p j c", j=PACK)
-        nc.sync.dma_start(w1_raw[:, 0, :], w1_rows[:, 0, :])
-        nc.scalar.dma_start(hsc_sb[:], hsc.rearrange("(p t) o -> p (t o)", t=PACK))
-        nc.sync.dma_start(offs_sb[:], offs)
+        keys_rows = keys_words[0].rearrange("p n t -> p (n t)").bitcast(I32)
+        key_cols = [slice(a, b) for a, b in zip(KEY_LOADS, KEY_LOADS[1:])]
+        nc.sync.dma_start(query_raw[:], query.rearrange("(p j) c -> p j c", j=PACK))
         nc.scalar.dma_start(sharp_sb[:], sharp)
+        nc.sync.dma_start(offs_sb[:], offs)
+        nc.scalar.dma_start(hsc_sb[:], hsc.rearrange("(p t) o -> p (t o)", t=PACK))
         nc.sync.dma_start(offs2_sb[:], offs2)
-        for j in range(1, PACK):
-            nc.sync.dma_start(w1_raw[:, j, :], w1_rows[:, j, :])
+        for cols in key_cols:
+            nc.sync.dma_start(key_words[:, cols], keys_rows[:, cols])
+        for f in range(4):
+            nc.sync.dma_start(key_scales[f:P:32, :].bitcast(I32), keys_scales[0, f:16:4, :].bitcast(I32))
+        nc.sync.dma_start(w1_raw[:], w1.rearrange("(p j) c -> p j c", j=PACK))
         for f in range(4):
             nc.sync.dma_start(
                 tab_scales_sb[TAB_PLANE_ROW + f : P : 32, :].bitcast(I32), tab_scales[0, f:16:4, :].bitcast(I32)
             )
+        nc.sync.dma_start(gates[0][:], gtab_planes[0])
         nc.sync.dma_start(tab_words_sb[:], tab_words[0].rearrange("p n t -> p (n t)").bitcast(I32))
-        for f in range(4):
-            nc.sync.dma_start(key_scales[f:P:32, :].bitcast(I32), keys_scales[0, f:16:4, :].bitcast(I32))
-        for t in range(PACK):
+        for t in range(1, PACK):
             nc.sync.dma_start(gates[t][:], gtab_planes[t])
         nc.sync.dma_start(gout_raw[:], gout.rearrange("(p j) c -> p j c", j=PACK))
-        nc.sync.dma_start(query_raw[:], query.rearrange("(p j) c -> p j c", j=PACK))
-        nc.sync.dma_start(key_words[:], keys_words[0].rearrange("p n t -> p (n t)").bitcast(I32))
         nc.sync.dma_start(old_sb[:], old)
+
+        halves = [slice(h * HALF, (h + 1) * HALF) for h in range(2)]
+        group_halves = [slice(h * G // 2, (h + 1) * G // 2) for h in range(2)]
+        both = list(zip(halves, group_halves))
+
+        def listed(offsets, slots):
+            return offsets[:, slots.start // 16 : slots.stop // 16]
 
         sharp8 = tile("sharp8", [P, 1], F32)
         neg_sharp8 = tile("neg_sharp8", [P, 1], F32)
         nc.scalar.activation(sharp8[:], sharp_sb[:], ACT.Copy, scale=1.0 / GROUP)
         nc.scalar.activation(neg_sharp8[:], sharp_sb[:], ACT.Copy, scale=-1.0 / GROUP)
 
+        query_bf = tile("query_bf", [P, Q, PACK], BF16)
+        nc.scalar.copy(query_bf[:], query_raw[:].rearrange("p j c -> p c j"))
+        query_codes, query_scales = quantize("query", query_bf[:].rearrange("p c j -> p (c j)"), Q)
+        key_w = tile("key_w", [P, I], U32)
+        nc.vector.tensor_copy(key_w[:], key_words[:].bitcast(U32).indirect(offs_sb[:]))
+        a_ps = []
+        for h in range(2):
+            key_s = tile("key_s%d" % h, [P, HALF], U8)
+            nc.vector.tensor_copy(key_s[:], key_scales[:].indirect(listed(offs_sb, halves[h])))
+            a_ps.append(ps.tile([P, HALF], F32, name="a_ps%d" % h))
+            nc.tensor.matmul_mx(
+                out=a_ps[h][:], lhsT=query_codes[:].bitcast(FP8X4), lhsT_scale=query_scales[:],
+                rhs=key_w[:, halves[h]].bitcast(FP8X4), rhs_scale=key_s[:], start=True, stop=True,
+            )
+        a_sum = tile("a_sum", [P, G], F32)
+        p_sb = tile("p_sb", [P, I], F32)
+        d = tile("d", [P, I], F32)
+        m = tile("m", [P, G], F32)
+        y = tile("y", [P, I], F32)
+        inner = tile("inner", [P, I], F32)
+        for h, (slots, groups) in enumerate(both):
+            nc.vector.tensor_reduce(a_sum[:, groups], by_group(a_ps[h][:]), AXIS_X, ALU.add)
+            nc.scalar.activation(p_sb[:, slots], a_ps[h][:], ACT.Exp)
+        neg_ms = tile("neg_ms", [P, G], F32)
+        neg_max = tile("neg_max", [P, 1], F32)
+        nc.vector.tensor_scalar(neg_ms[:], a_sum[:], neg_sharp8[:], None, ALU.mult, ALU.min, accum_out=neg_max[:])
+        pg = tile("pg", [P, G], F32)
+        z = tile("z", [P, 1], F32)
+        nc.scalar.activation(pg[:], neg_ms[:], ACT.Exp, bias=neg_max[:], scale=-1.0, accum_out=z[:])
+
         w1_bf = tile("w1_bf", [P, PACK, P, PACK], BF16)
-        nc.scalar.activation(
-            w1_bf[:].rearrange("p t m j -> p m t j"), w1_raw[:].rearrange("p j (m t) -> p m t j", t=PACK), ACT.Copy
+        nc.gpsimd.tensor_scalar(
+            w1_bf[:].rearrange("p t m j -> p m t j"), w1_raw[:].rearrange("p j (m t) -> p m t j", t=PACK),
+            1.0, 0.0, ALU.mult, ALU.add,
         )
-        tab_w = tile("tab_w", [P, I], U32)
-        tab_s = tile("tab_s", [P, I], U8)
+        tab_s = tile("tab_s", [P, I], U8, tag="a_sum")
         nc.vector.tensor_copy(tab_s[:], tab_scales_sb[:].indirect(offs_sb[:]))
+        s = tile("s", [P, G], F32)
+        nc.vector.tensor_reduce(s[:], by_group(p_sb[:]), AXIS_X, ALU.add)
+        w1_codes, w1_scales = quantize("w1", w1_bf[:].rearrange("p t m j -> p (t m j)"), R, "tab_scales_sb")
+        tab_w = tile("tab_w", [P, I], U32, tag="w1_bf")
         nc.vector.tensor_copy(tab_w[:], tab_words_sb[:].bitcast(U32).indirect(offs_sb[:]))
-        w1_codes, w1_scales = quantize("w1", w1_bf[:].rearrange("p t m j -> p (t m j)"), R, "tab_words_sb")
         zh = [ps.tile([P, I], F32, name="zh%d" % t) for t in range(PACK)]
         for t in range(PACK):
             cols = slice(t * P, (t + 1) * P)
@@ -108,82 +152,54 @@ def tile_attend_blrgated_bygroup_kernel(
                 out=zh[t][:], lhsT=w1_codes[:, cols].bitcast(FP8X4), lhsT_scale=w1_scales[:, cols],
                 rhs=tab_w[:].bitcast(FP8X4), rhs_scale=tab_s[TAB_PLANE_ROW:P, :], start=True, stop=True,
             )
-
-        pairs = tile("pairs", [P, 2, I, 2], BF16)
-        for t in range(PACK):
-            hg = tile("hg%d" % t, [P, I], F32)
-            nc.scalar.activation(hg[:], gates[t][:].indirect(offs2_sb[:]), ACT.Sigmoid)
-            nc.vector.scalar_tensor_tensor(
-                pairs[:, t // 2, :, t % 2], zh[t][:], hsc_sb[:, t : t + 1], hg[:], ALU.mult, ALU.mult
-            )
-        window = tile("window", [P, T], F32, tag="gates0")
-        nc.gpsimd.memset(window[:], 0.0)
-        key_s = tile("key_s", [P, I], U8, tag="w1_bf")
-        nc.vector.tensor_copy(key_s[:], key_scales[:].indirect(offs_sb[:]))
-
-        hs_words = tile("hs_words", [P, I, 2], I32)
-        pair_words = pairs[:].rearrange("p a n e -> p (a n e)").bitcast(I32)
-        nc.vector.tensor_copy(hs_words[:], pair_words.rearrange("p (a n) -> p n a", a=2))
-        hs_codes, hs_scales = quantize("hs", hs_words[:].rearrange("p n a -> p (n a)").bitcast(BF16), I)
-
-        gout_bf = tile("gout_bf", [P, Q, PACK], BF16, tag="gates1")
-        nc.gpsimd.tensor_scalar(gout_bf[:], gout_raw[:].rearrange("p j c -> p c j"), 1.0, 0.0, ALU.mult, ALU.add)
-        query_bf = tile("query_bf", [P, Q, PACK], BF16, tag="gout_raw")
-        nc.gpsimd.tensor_scalar(query_bf[:], query_raw[:].rearrange("p j c -> p c j"), 1.0, 0.0, ALU.mult, ALU.add)
-        gout_codes, gout_scales = quantize("gout", gout_bf[:].rearrange("p c j -> p (c j)"), Q, "hg3")
-        query_codes, query_scales = quantize("query", query_bf[:].rearrange("p c j -> p (c j)"), Q, "hg2")
-        c0 = ps.tile([P, I], F32, name="c0")
-        nc.tensor.matmul_mx(
-            out=c0[:], lhsT=gout_codes[:].bitcast(FP8X4), lhsT_scale=gout_scales[:],
-            rhs=hs_codes[:].bitcast(FP8X4), rhs_scale=hs_scales[:], start=True, stop=True,
-        )
-
-        halves = [slice(h * HALF, (h + 1) * HALF) for h in range(2)]
-        group_halves = [slice(h * G // 2, (h + 1) * G // 2) for h in range(2)]
-        a_ps = []
-        for h, tag in enumerate(("pairs", "hs_words")):
-            key_w = tile("key_w%d" % h, [P, HALF], U32, tag=tag)
-            listed = offs_sb[:, h * HALF // 16 : (h + 1) * HALF // 16]
-            nc.vector.tensor_copy(key_w[:], key_words[:].bitcast(U32).indirect(listed))
-            a_ps.append(ps.tile([P, HALF], F32, name="a_ps%d" % h))
-            nc.tensor.matmul_mx(
-                out=a_ps[h][:], lhsT=query_codes[:].bitcast(FP8X4), lhsT_scale=query_scales[:],
-                rhs=key_w[:].bitcast(FP8X4), rhs_scale=key_s[:, halves[h]], start=True, stop=True,
-            )
-        a_sum = tile("a_sum", [P, G], F32)
-        p_sb = tile("p_sb", [P, I], F32)
-        s = tile("s", [P, G], F32)
-        inv_s = tile("inv_s", [P, G], F32)
-        pn = tile("pn", [P, I], F32)
-        d = tile("d", [P, I], F32)
-        m = tile("m", [P, G], F32)
-        y = tile("y", [P, I], F32)
-        inner = tile("inner", [P, I], F32)
-        both = list(zip(halves, group_halves))
-        for h, (slots, groups) in enumerate(both):
-            nc.scalar.activation(p_sb[:, slots], a_ps[h][:], ACT.Exp)
-            nc.vector.tensor_reduce(a_sum[:, groups], by_group(a_ps[h][:]), AXIS_X, ALU.add)
-        neg_ms = tile("neg_ms", [P, G], F32)
-        neg_max = tile("neg_max", [P, 1], F32)
-        nc.vector.tensor_reduce(s[:, group_halves[0]], by_group(p_sb[:, halves[0]]), AXIS_X, ALU.add)
-        nc.vector.tensor_scalar(neg_ms[:], a_sum[:], neg_sharp8[:], None, ALU.mult, ALU.min, accum_out=neg_max[:])
-        nc.vector.tensor_reduce(s[:, group_halves[1]], by_group(p_sb[:, halves[1]]), AXIS_X, ALU.add)
-        pg = tile("pg", [P, G], F32)
-        z = tile("z", [P, 1], F32)
-        nc.scalar.activation(pg[:], neg_ms[:], ACT.Exp, bias=neg_max[:], scale=-1.0, accum_out=z[:])
+        inv_s = tile("inv_s", [P, G], F32, tag="tab_words_sb")
         inv_z = tile("inv_z", [P, 1], F32)
-        for slots, groups in both:
-            nc.vector.reciprocal(inv_s[:, groups], s[:, groups])
+        nc.vector.reciprocal(inv_s[:], s[:])
         nc.vector.reciprocal(inv_z[:], z[:])
-        w_slots = tile("w_slots", [P, I], F32)
+        pn = tile("pn", [P, I], F32)
+        nc.gpsimd.tensor_tensor(by_group(pn[:]), by_group(p_sb[:]), spread(inv_s[:], G), ALU.mult)
+
+        pairs = tile("pairs", [P, 2, 2, HALF, 2], BF16)
+
+        def gate(t, slots, tag=None):
+            hg = tile("hg%d_%d" % (t, slots.start), [P, slots.stop - slots.start], F32, tag=tag)
+            nc.scalar.activation(hg[:], gates[t][:].indirect(listed(offs2_sb, slots)), ACT.Sigmoid)
+            return hg
+
+        def by_half(ap):
+            return ap.rearrange("p (h n) -> p h n", h=2)
+
+        for t in range(PACK - 1):
+            hg = gate(t, slice(0, I), tag="neg_ms" if t == 0 else None)
+            nc.vector.scalar_tensor_tensor(
+                pairs[:, :, t // 2, :, t % 2], by_half(zh[t][:]), hsc_sb[:, t : t + 1], by_half(hg[:]), ALU.mult, ALU.mult
+            )
+        gout_bf = tile("gout_bf", [P, Q, PACK], BF16, tag="gates2")
+        nc.gpsimd.tensor_scalar(gout_bf[:], gout_raw[:].rearrange("p j c -> p c j"), 1.0, 0.0, ALU.mult, ALU.add)
+        t = PACK - 1
+        for h in range(2):
+            hg = gate(t, halves[h])
+            nc.vector.scalar_tensor_tensor(
+                pairs[:, h, t // 2, :, t % 2], zh[t][:, halves[h]], hsc_sb[:, t : t + 1], hg[:], ALU.mult, ALU.mult
+            )
+        hs_words = [tile("hs_words%d" % h, [P, HALF, 2], I32) for h in range(2)]
+        pair_words = pairs[:].rearrange("p h a n e -> p (h a n e)").bitcast(I32).rearrange("p (h a n) -> p h n a", h=2, a=2)
+        for h in range(2):
+            nc.vector.tensor_copy(hs_words[h][:], pair_words[:, h])
+        w_slots = tile("w_slots", [P, I], F32, tag="gates3")
         nc.scalar.activation(by_group(w_slots[:]), spread(pg[:], G), ACT.Copy, scale=inv_z[:])
-        for slots, groups in both:
-            nc.vector.tensor_tensor(
-                by_group(pn[:, slots]), by_group(p_sb[:, slots]), spread(inv_s[:, groups], G // 2), ALU.mult
+        gout_codes, gout_scales = quantize("gout", gout_bf[:].rearrange("p c j -> p (c j)"), Q)
+        c0 = []
+        for h in range(2):
+            hs_codes, hs_scales = quantize("hs%d" % h, hs_words[h][:].rearrange("p n a -> p (n a)").bitcast(BF16), HALF)
+            c0.append(ps.tile([P, HALF], F32, name="c0_%d" % h))
+            nc.tensor.matmul_mx(
+                out=c0[h][:], lhsT=gout_codes[:].bitcast(FP8X4), lhsT_scale=gout_scales[:],
+                rhs=hs_codes[:].bitcast(FP8X4), rhs_scale=hs_scales[:], start=True, stop=True,
             )
 
-        for slots, groups in both:
-            nc.vector.scalar_tensor_tensor(d[:, slots], c0[:, slots], -512.0, pn[:, slots], ALU.mult, ALU.mult)
+        for h in range(2):
+            nc.vector.scalar_tensor_tensor(d[:, halves[h]], c0[h][:], -512.0, pn[:, halves[h]], ALU.mult, ALU.mult)
         for slots, groups in both:
             nc.vector.tensor_reduce(m[:, groups], by_group(d[:, slots]), AXIS_X, ALU.add)
         wm = tile("wm", [P, G], F32)

@@ -130,8 +130,8 @@ def tile_attend_blrgated_bygroup_kernel(
         neg_max = tile("neg_max", [P, 1], F32)
         nc.vector.tensor_scalar(neg_ms[:], a_sum[:], neg_sharp8[:], None, ALU.mult, ALU.min, accum_out=neg_max[:])
         pg = tile("pg", [P, G], F32)
-        z = tile("z", [P, 1], F32)
-        nc.scalar.activation(pg[:], neg_ms[:], ACT.Exp, bias=neg_max[:], scale=-1.0, accum_out=z[:])
+        sums = tile("sums", [P, G + 1], F32)
+        nc.scalar.activation(pg[:], neg_ms[:], ACT.Exp, bias=neg_max[:], scale=-1.0, accum_out=sums[:, G : G + 1])
 
         w1_bf = tile("w1_bf", [P, PACK, P, PACK], BF16)
         nc.gpsimd.tensor_scalar(
@@ -140,8 +140,7 @@ def tile_attend_blrgated_bygroup_kernel(
         )
         tab_s = tile("tab_s", [P, I], U8, tag="a_sum")
         nc.vector.tensor_copy(tab_s[:], tab_scales_sb[:].indirect(offs_sb[:]))
-        s = tile("s", [P, G], F32)
-        nc.vector.tensor_reduce(s[:], by_group(p_sb[:]), AXIS_X, ALU.add)
+        nc.vector.tensor_reduce(sums[:, 0:G], by_group(p_sb[:]), AXIS_X, ALU.add)
         w1_codes, w1_scales = quantize("w1", w1_bf[:].rearrange("p t m j -> p (t m j)"), R, "tab_scales_sb")
         tab_w = tile("tab_w", [P, I], U32, tag="w1_bf")
         nc.vector.tensor_copy(tab_w[:], tab_words_sb[:].bitcast(U32).indirect(offs_sb[:]))
@@ -152,42 +151,43 @@ def tile_attend_blrgated_bygroup_kernel(
                 out=zh[t][:], lhsT=w1_codes[:, cols].bitcast(FP8X4), lhsT_scale=w1_scales[:, cols],
                 rhs=tab_w[:].bitcast(FP8X4), rhs_scale=tab_s[TAB_PLANE_ROW:P, :], start=True, stop=True,
             )
-        inv_s = tile("inv_s", [P, G], F32, tag="tab_words_sb")
-        inv_z = tile("inv_z", [P, 1], F32)
-        nc.vector.reciprocal(inv_s[:], s[:])
-        nc.vector.reciprocal(inv_z[:], z[:])
+        inverses = tile("inverses", [P, G + 1], F32, tag="tab_words_sb")
+        nc.vector.reciprocal(inverses[:], sums[:])
         pn = tile("pn", [P, I], F32)
-        nc.gpsimd.tensor_tensor(by_group(pn[:]), by_group(p_sb[:]), spread(inv_s[:], G), ALU.mult)
+        nc.gpsimd.tensor_tensor(by_group(pn[:]), by_group(p_sb[:]), spread(inverses[:, 0:G], G), ALU.mult)
 
-        pairs = tile("pairs", [P, 2, 2, HALF, 2], BF16)
+        first_planes = tile("first_planes", [P, 2, I], BF16)
+        pairs = [tile("pairs%d" % h, [P, 2, HALF, 2], BF16) for h in range(2)]
 
         def gate(t, slots, tag=None):
             hg = tile("hg%d_%d" % (t, slots.start), [P, slots.stop - slots.start], F32, tag=tag)
             nc.scalar.activation(hg[:], gates[t][:].indirect(listed(offs2_sb, slots)), ACT.Sigmoid)
             return hg
 
-        def by_half(ap):
-            return ap.rearrange("p (h n) -> p h n", h=2)
+        def scale_and_gate(dst, t, slots, hg):
+            nc.vector.scalar_tensor_tensor(dst, zh[t][:, slots], hsc_sb[:, t : t + 1], hg, ALU.mult, ALU.mult)
 
-        for t in range(PACK - 1):
+        for t in range(2):
             hg = gate(t, slice(0, I), tag="neg_ms" if t == 0 else None)
-            nc.vector.scalar_tensor_tensor(
-                pairs[:, :, t // 2, :, t % 2], by_half(zh[t][:]), hsc_sb[:, t : t + 1], by_half(hg[:]), ALU.mult, ALU.mult
-            )
-        gout_bf = tile("gout_bf", [P, Q, PACK], BF16, tag="gates2")
-        nc.gpsimd.tensor_scalar(gout_bf[:], gout_raw[:].rearrange("p j c -> p c j"), 1.0, 0.0, ALU.mult, ALU.add)
-        t = PACK - 1
+            scale_and_gate(first_planes[:, t, :], t, slice(0, I), hg[:])
         for h in range(2):
-            hg = gate(t, halves[h])
-            nc.vector.scalar_tensor_tensor(
-                pairs[:, h, t // 2, :, t % 2], zh[t][:, halves[h]], hsc_sb[:, t : t + 1], hg[:], ALU.mult, ALU.mult
+            nc.gpsimd.tensor_scalar(
+                pairs[h][:, 0], first_planes[:, :, halves[h]].rearrange("p e n -> p n e"), 1.0, 0.0, ALU.mult, ALU.add
             )
-        hs_words = [tile("hs_words%d" % h, [P, HALF, 2], I32) for h in range(2)]
-        pair_words = pairs[:].rearrange("p h a n e -> p (h a n e)").bitcast(I32).rearrange("p (h a n) -> p h n a", h=2, a=2)
+        hg = gate(2, slice(0, I))
         for h in range(2):
-            nc.vector.tensor_copy(hs_words[h][:], pair_words[:, h])
-        w_slots = tile("w_slots", [P, I], F32, tag="gates3")
-        nc.scalar.activation(by_group(w_slots[:]), spread(pg[:], G), ACT.Copy, scale=inv_z[:])
+            scale_and_gate(pairs[h][:, 1, :, 0], 2, halves[h], hg[:, halves[h]])
+        for h in range(2):
+            hg = gate(3, halves[h])
+            scale_and_gate(pairs[h][:, 1, :, 1], 3, halves[h], hg[:])
+        gout_bf = tile("gout_bf", [P, Q, PACK], BF16, tag="gates3")
+        nc.scalar.copy(gout_bf[:], gout_raw[:].rearrange("p j c -> p c j"))
+        hs_words = [tile("hs_words%d" % h, [P, HALF, 2], U32) for h in range(2)]
+        for h in range(2):
+            pair_words = pairs[h][:].rearrange("p a n e -> p (a n e)").bitcast(U32)
+            nc.scalar.copy(hs_words[h][:], pair_words.rearrange("p (a n) -> p n a", a=2))
+        w_slots = tile("w_slots", [P, I], F32, tag="pairs1")
+        nc.scalar.activation(by_group(w_slots[:]), spread(pg[:], G), ACT.Copy, scale=inverses[:, G : G + 1])
         gout_codes, gout_scales = quantize("gout", gout_bf[:].rearrange("p c j -> p (c j)"), Q)
         c0 = []
         for h in range(2):

from contextlib import ExitStack

import concourse.mybir as mybir

F32 = mybir.dt.float32
BF16 = mybir.dt.bfloat16
I32 = mybir.dt.int32
U32 = mybir.dt.uint32
U16 = mybir.dt.uint16
U8 = mybir.dt.uint8
FP8X4 = mybir.dt.float8_e4m3fn_x4
ALU = mybir.AluOpType
ACT = mybir.ActivationFunctionType
AXIS_X = mybir.AxisListType.X

P = 128
PACK = 4
D, K, R, T, I, Q, G, U = 512, 512, 512, 2048, 512, 128, 64, 1024
GROUP = I // G
HALF = I // 2
OUT_CHUNKS = (640, 640, 512, 256)
KEY_LOADS = (0, 768, 1408, 2048)
TAB_PLANE_ROW = 4

FLOPS = 2 * (D * Q * I + K * R * I + R * Q * I)


def tile_attend_blrgated_bygroup_kernel(
    tc, query, keys_words, keys_scales, sharp, tab_words, tab_scales, w1, gtab, gout, hsc, old, offs2, offs, out
):
    nc = tc.nc
    with ExitStack() as ctx:
        sb = ctx.enter_context(tc.tile_pool(name="sb", bufs=1))
        ps = ctx.enter_context(tc.psum_pool(name="ps", bufs=1))

        def tile(name, shape, dtype, tag=None):
            return sb.tile(shape, dtype, name=name, tag=tag or name, align_bytes=64)

        def by_group(ap):
            return ap.rearrange("p (g j) -> p g j", j=GROUP)

        def spread(ap, groups):
            return ap.unsqueeze(2).to_broadcast([P, groups, GROUP])

        def quantize(name, grouped, width, tag=None):
            codes = tile(name + "_codes", [P, width], U32, tag=tag)
            scales = tile(name + "_scales", [P, width], U8)
            nc.vector.quantize_mx(out=codes[:].bitcast(FP8X4), scales=scales[:], in_=grouped)
            return codes, scales

        offs_sb = sb.tile([P, I // 16], U16, name="offs_sb")
        offs2_sb = sb.tile([P, I // 16], U16, name="offs2_sb")
        key_words = tile("key_words", [P, T], I32)
        tab_words_sb = tile("tab_words_sb", [P, T], I32)
        key_scales = tile("key_scales", [P, T], U8)
        tab_scales_sb = tile("tab_scales_sb", [P, T], U8)
        query_raw = tile("query_raw", [P, PACK, Q], F32)
        gout_raw = tile("gout_raw", [P, PACK, Q], F32)
        w1_raw = tile("w1_raw", [P, PACK, R], F32)
        gates = [tile("gates%d" % t, [P, U], F32) for t in range(PACK)]
        old_sb = tile("old_sb", [P, T], F32)
        sharp_sb = tile("sharp_sb", [P, 1], F32)
        hsc_sb = tile("hsc_sb", [P, PACK], F32)

        window = tile("window", [P, T], F32)
        nc.vector.memset(key_scales[:].bitcast(I32), 0)
        nc.vector.memset(tab_scales_sb[:].bitcast(I32), 0)
        nc.vector.memset(window[:], 0.0)

        gtab_planes = gtab.rearrange("(p t) u -> t p u", t=PACK)
        keys_rows = keys_words[0].rearrange("p n t -> p (n t)").bitcast(I32)
        key_cols = [slice(a, b) for a, b in zip(KEY_LOADS, KEY_LOADS[1:])]
        nc.sync.dma_start(query_raw[:], query.rearrange("(p j) c -> p j c", j=PACK))
        nc.scalar.dma_start(sharp_sb[:], sharp)
        nc.sync.dma_start(offs_sb[:], offs)
        nc.scalar.dma_start(hsc_sb[:], hsc.rearrange("(p t) o -> p (t o)", t=PACK))
        nc.sync.dma_start(offs2_sb[:], offs2)
        for cols in key_cols:
            nc.sync.dma_start(key_words[:, cols], keys_rows[:, cols])
        for f in range(4):
            nc.sync.dma_start(key_scales[f:P:32, :].bitcast(I32), keys_scales[0, f:16:4, :].bitcast(I32))
        nc.sync.dma_start(w1_raw[:], w1.rearrange("(p j) c -> p j c", j=PACK))
        for f in range(4):
            nc.sync.dma_start(
                tab_scales_sb[TAB_PLANE_ROW + f : P : 32, :].bitcast(I32), tab_scales[0, f:16:4, :].bitcast(I32)
            )
        nc.sync.dma_start(gates[0][:], gtab_planes[0])
        nc.sync.dma_start(tab_words_sb[:], tab_words[0].rearrange("p n t -> p (n t)").bitcast(I32))
        for t in range(1, PACK):
            nc.sync.dma_start(gates[t][:], gtab_planes[t])
        nc.sync.dma_start(gout_raw[:], gout.rearrange("(p j) c -> p j c", j=PACK))
        nc.sync.dma_start(old_sb[:], old)

        halves = [slice(h * HALF, (h + 1) * HALF) for h in range(2)]
        group_halves = [slice(h * G // 2, (h + 1) * G // 2) for h in range(2)]
        both = list(zip(halves, group_halves))

        def listed(offsets, slots):
            return offsets[:, slots.start // 16 : slots.stop // 16]

        sharp8 = tile("sharp8", [P, 1], F32)
        neg_sharp8 = tile("neg_sharp8", [P, 1], F32)
        nc.scalar.activation(sharp8[:], sharp_sb[:], ACT.Copy, scale=1.0 / GROUP)
        nc.scalar.activation(neg_sharp8[:], sharp_sb[:], ACT.Copy, scale=-1.0 / GROUP)

        query_bf = tile("query_bf", [P, Q, PACK], BF16)
        nc.scalar.copy(query_bf[:], query_raw[:].rearrange("p j c -> p c j"))
        query_codes, query_scales = quantize("query", query_bf[:].rearrange("p c j -> p (c j)"), Q)
        key_w = tile("key_w", [P, I], U32)
        nc.vector.tensor_copy(key_w[:], key_words[:].bitcast(U32).indirect(offs_sb[:]))
        a_ps = []
        for h in range(2):
            key_s = tile("key_s%d" % h, [P, HALF], U8)
            nc.vector.tensor_copy(key_s[:], key_scales[:].indirect(listed(offs_sb, halves[h])))
            a_ps.append(ps.tile([P, HALF], F32, name="a_ps%d" % h))
            nc.tensor.matmul_mx(
                out=a_ps[h][:], lhsT=query_codes[:].bitcast(FP8X4), lhsT_scale=query_scales[:],
                rhs=key_w[:, halves[h]].bitcast(FP8X4), rhs_scale=key_s[:], start=True, stop=True,
            )
        a_sum = tile("a_sum", [P, G], F32)
        p_sb = tile("p_sb", [P, I], F32)
        d = tile("d", [P, I], F32)
        m = tile("m", [P, G], F32)
        y = tile("y", [P, I], F32)
        inner = tile("inner", [P, I], F32)
        for h, (slots, groups) in enumerate(both):
            nc.vector.tensor_reduce(a_sum[:, groups], by_group(a_ps[h][:]), AXIS_X, ALU.add)
            nc.scalar.activation(p_sb[:, slots], a_ps[h][:], ACT.Exp)
        neg_ms = tile("neg_ms", [P, G], F32)
        neg_max = tile("neg_max", [P, 1], F32)
        nc.vector.tensor_scalar(neg_ms[:], a_sum[:], neg_sharp8[:], None, ALU.mult, ALU.min, accum_out=neg_max[:])
        pg = tile("pg", [P, G], F32)
        sums = tile("sums", [P, G + 1], F32)
        nc.scalar.activation(pg[:], neg_ms[:], ACT.Exp, bias=neg_max[:], scale=-1.0, accum_out=sums[:, G : G + 1])

        w1_bf = tile("w1_bf", [P, PACK, P, PACK], BF16)
        nc.gpsimd.tensor_scalar(
            w1_bf[:].rearrange("p t m j -> p m t j"), w1_raw[:].rearrange("p j (m t) -> p m t j", t=PACK),
            1.0, 0.0, ALU.mult, ALU.add,
        )
        tab_s = tile("tab_s", [P, I], U8, tag="a_sum")
        nc.vector.tensor_copy(tab_s[:], tab_scales_sb[:].indirect(offs_sb[:]))
        nc.vector.tensor_reduce(sums[:, 0:G], by_group(p_sb[:]), AXIS_X, ALU.add)
        w1_codes, w1_scales = quantize("w1", w1_bf[:].rearrange("p t m j -> p (t m j)"), R, "tab_scales_sb")
        tab_w = tile("tab_w", [P, I], U32, tag="w1_bf")
        nc.vector.tensor_copy(tab_w[:], tab_words_sb[:].bitcast(U32).indirect(offs_sb[:]))
        zh = [ps.tile([P, I], F32, name="zh%d" % t) for t in range(PACK)]
        for t in range(PACK):
            cols = slice(t * P, (t + 1) * P)
            nc.tensor.matmul_mx(
                out=zh[t][:], lhsT=w1_codes[:, cols].bitcast(FP8X4), lhsT_scale=w1_scales[:, cols],
                rhs=tab_w[:].bitcast(FP8X4), rhs_scale=tab_s[TAB_PLANE_ROW:P, :], start=True, stop=True,
            )
        inverses = tile("inverses", [P, G + 1], F32, tag="tab_words_sb")
        nc.vector.reciprocal(inverses[:], sums[:])
        pn = tile("pn", [P, I], F32)
        nc.gpsimd.tensor_tensor(by_group(pn[:]), by_group(p_sb[:]), spread(inverses[:, 0:G], G), ALU.mult)

        first_planes = tile("first_planes", [P, 2, I], BF16)
        pairs = [tile("pairs%d" % h, [P, 2, HALF, 2], BF16) for h in range(2)]

        def gate(t, slots, tag=None):
            hg = tile("hg%d_%d" % (t, slots.start), [P, slots.stop - slots.start], F32, tag=tag)
            nc.scalar.activation(hg[:], gates[t][:].indirect(listed(offs2_sb, slots)), ACT.Sigmoid)
            return hg

        def scale_and_gate(dst, t, slots, hg):
            nc.vector.scalar_tensor_tensor(dst, zh[t][:, slots], hsc_sb[:, t : t + 1], hg, ALU.mult, ALU.mult)

        for t in range(2):
            hg = gate(t, slice(0, I), tag="neg_ms" if t == 0 else None)
            scale_and_gate(first_planes[:, t, :], t, slice(0, I), hg[:])
        for h in range(2):
            nc.gpsimd.tensor_scalar(
                pairs[h][:, 0], first_planes[:, :, halves[h]].rearrange("p e n -> p n e"), 1.0, 0.0, ALU.mult, ALU.add
            )
        hg = gate(2, slice(0, I))
        for h in range(2):
            scale_and_gate(pairs[h][:, 1, :, 0], 2, halves[h], hg[:, halves[h]])
        for h in range(2):
            hg = gate(3, halves[h])
            scale_and_gate(pairs[h][:, 1, :, 1], 3, halves[h], hg[:])
        gout_bf = tile("gout_bf", [P, Q, PACK], BF16, tag="gates3")
        nc.scalar.copy(gout_bf[:], gout_raw[:].rearrange("p j c -> p c j"))
        hs_words = [tile("hs_words%d" % h, [P, HALF, 2], U32) for h in range(2)]
        for h in range(2):
            pair_words = pairs[h][:].rearrange("p a n e -> p (a n e)").bitcast(U32)
            nc.scalar.copy(hs_words[h][:], pair_words.rearrange("p (a n) -> p n a", a=2))
        w_slots = tile("w_slots", [P, I], F32, tag="pairs1")
        nc.scalar.activation(by_group(w_slots[:]), spread(pg[:], G), ACT.Copy, scale=inverses[:, G : G + 1])
        gout_codes, gout_scales = quantize("gout", gout_bf[:].rearrange("p c j -> p (c j)"), Q)
        c0 = []
        for h in range(2):
            hs_codes, hs_scales = quantize("hs%d" % h, hs_words[h][:].rearrange("p n a -> p (n a)").bitcast(BF16), HALF)
            c0.append(ps.tile([P, HALF], F32, name="c0_%d" % h))
            nc.tensor.matmul_mx(
                out=c0[h][:], lhsT=gout_codes[:].bitcast(FP8X4), lhsT_scale=gout_scales[:],
                rhs=hs_codes[:].bitcast(FP8X4), rhs_scale=hs_scales[:], start=True, stop=True,
            )

        for h in range(2):
            nc.vector.scalar_tensor_tensor(d[:, halves[h]], c0[h][:], -512.0, pn[:, halves[h]], ALU.mult, ALU.mult)
        for slots, groups in both:
            nc.vector.tensor_reduce(m[:, groups], by_group(d[:, slots]), AXIS_X, ALU.add)
        wm = tile("wm", [P, G], F32)
        mean8 = tile("mean8", [P, 1], F32)

        def centre(slots, groups):
            nc.vector.scalar_tensor_tensor(
                by_group(y[:, slots]), by_group(pn[:, slots]), sharp8[:], spread(m[:, groups], G // 2),
                ALU.subtract, ALU.mult,
            )

        centre(*both[0])
        nc.vector.scalar_tensor_tensor(
            wm[:], m[:], sharp8[:], w_slots[:, 0:I:GROUP], ALU.mult, ALU.mult, accum_out=mean8[:]
        )
        centre(*both[1])
        for slots, groups in both:
            nc.vector.scalar_tensor_tensor(inner[:, slots], y[:, slots], mean8[:], d[:, slots], ALU.add, ALU.subtract)
        nc.vector.tensor_tensor(window[:].indirect(offs_sb[:]), inner[:], w_slots[:], ALU.mult)

        start = 0
        for c, width in enumerate(OUT_CHUNKS):
            cols = slice(start, start + width)
            start = start + width
            result = tile("result%d" % c, [P, width], F32)
            nc.vector.tensor_tensor(result[:], window[:, cols], old_sb[:, cols], ALU.add)
            queue = nc.sync if c % 2 == 0 else nc.scalar
            queue.dma_start(out[:, cols], result[:])
